import numpy as np
import ml_dtypes


def mxq(x, axis, fmt="e4m3"):
    dtype, down = {"e4m3": (ml_dtypes.float8_e4m3fn, 7), "e5m2": (ml_dtypes.float8_e5m2, 14)}[fmt]
    v = np.moveaxis(np.asarray(x, np.float32).astype(ml_dtypes.bfloat16).astype(np.float64), axis, -1)
    blocks = v.reshape(v.shape[:-1] + (-1, 32))
    amax = np.abs(blocks).max(-1, keepdims=True)
    byte = np.maximum(np.where(amax > 0, np.frexp(amax)[1] - 1 + 127, 0) - down, 1)
    scale = np.exp2(byte - 127.0)
    codes = (blocks / scale).astype(np.float32).astype(dtype).astype(np.float64)
    return np.moveaxis((codes * scale).reshape(v.shape), -1, axis)


WIDE = False


def mx_kscale(k):
    if not WIDE:
        return np.ones(k)
    levels = np.array([10, -10, 5, -5, 0])
    if k % 512:
        return np.exp2(np.random.permutation(np.resize(levels, k // 32))).repeat(32)
    a = np.empty((k // 512, 16))
    for p in range(k // 512):
        a[p, :8] = np.random.permutation(np.resize(levels, 8))
        for g in range(8):
            far = levels[np.abs(levels - a[p, g]) >= 10]
            a[p, g + 8] = far[np.random.randint(len(far))]
    return np.exp2(a.ravel()).repeat(32)


def f64(x):
    return np.asarray(x).astype(np.float64)


def striped8(idx):
    return np.asarray(idx).reshape(8, -1, 16).transpose(0, 2, 1).reshape(128, -1).astype(np.uint16)


def unstriped8(offs):
    return offs.reshape(8, 16, -1).transpose(0, 2, 1).reshape(8, -1).astype(np.int64)


def pick8(x, idx, run):
    r = np.arange(len(x))
    return x[r[:, None], idx[r % (8 * run) // run]]


E2M1 = np.array([0.0, 0.5, 1.0, 1.5, 2.0, 3.0, 4.0, 6.0, -0.0, -0.5, -1.0, -1.5, -2.0, -3.0, -4.0, -6.0])


def pack_weight(w, fmt):
    k, n = w.shape
    w = f64(np.asarray(w, np.float32).astype(ml_dtypes.bfloat16)).reshape(k // 32, 32, n)
    amax = np.abs(w).max(1)
    if fmt == "e4m3":
        byte = np.frexp(amax)[1] - 1 + 127 - 7
    else:
        mant, ex = np.frexp(amax / 6.0)
        byte = np.where(mant > 0.5, ex, ex - 1) + 127
    byte = np.clip(np.where(amax > 0, byte, 1), 1, 254)
    scaled = (w * np.exp2(127.0 - byte)[:, None, :]).reshape(k, n).astype(np.float32)
    by_word = np.ascontiguousarray(scaled.reshape(k // 512, 128, 4, n).transpose(0, 1, 3, 2))
    if fmt == "e4m3":
        words = by_word.astype(ml_dtypes.float8_e4m3fn).view(np.uint8)
    else:
        c = by_word.astype(ml_dtypes.float4_e2m1fn).view(np.uint8) & 0xF
        words = (c[..., 0::2] | (c[..., 1::2] << 4)).reshape(k // 512, 128, 2 * n)
    return np.ascontiguousarray(words), np.ascontiguousarray(byte.astype(np.uint8).reshape(k // 512, 16, n))


def unpack_weight(words, scales, fmt):
    g, _, n = scales.shape
    words = np.ascontiguousarray(words).reshape(g, 128, n, -1)
    if fmt == "e4m3":
        vals = words.view(ml_dtypes.float8_e4m3fn).astype(np.float64)
    else:
        nib = np.empty((g, 128, n, 4), np.uint8)
        nib[..., 0::2] = words & 0xF
        nib[..., 1::2] = words >> 4
        vals = E2M1[nib]
    vals = vals * np.repeat(np.exp2(scales.astype(np.float64) - 127.0), 8, axis=1)[..., None]
    return vals.transpose(0, 1, 3, 2).reshape(g * 512, n)


D, V, Q, I = 512, 2048, 128, 1024


def setup_inputs():
    n = np.random.standard_normal
    idx = np.stack([np.random.permutation(V)[:I] for _ in range(8)])
    fd = mx_kscale(D)
    vocp = pack_weight(n((D, V)) / fd[:, None], "e2m1")
    return {
        "hid": (n((D, Q)) * 1.0 / np.sqrt(D) * fd[:, None]).astype(np.float32),
        "voc_words": vocp[0],
        "voc_scales": vocp[1],
        "fine": (np.random.uniform(8.0, 12.0, (Q, 1))).astype(np.float32),
        "offs": striped8(idx),
    }


def reference(hid, voc_words, voc_scales, fine, offs):
    idx = unstriped8(offs)
    vocu = unpack_weight(voc_words, voc_scales, "e2m1")
    hidq = mxq(f64(hid), 0, "e4m3")
    a = hidq.T @ vocu
    m1 = np.max(pick8(a, idx, 16), axis=1, keepdims=True)
    r = np.exp(pick8(a, idx, 16) - m1)
    up = f64(fine) - m1 - np.log(np.sum(r, axis=1, keepdims=True))
    dl = pick8(a, idx, 16) + up
    df = np.zeros((Q, V))
    df[np.arange(Q)[:, None], idx[np.arange(Q) % 128 // 16]] = dl
    y = df - f64(fine)
    return y

@@ -1,0 +1,163 @@
+import math
+from contextlib import ExitStack
+
+import concourse.mybir as mybir
+
+D, V, Q, LISTED = 512, 2048, 128, 1024
+FLOPS = 2 * D * V * Q
+
+F32 = mybir.dt.float32
+BF16 = mybir.dt.bfloat16
+I32 = mybir.dt.int32
+U32 = mybir.dt.uint32
+U16 = mybir.dt.uint16
+U8 = mybir.dt.uint8
+FP8X4 = mybir.dt.float8_e4m3fn_x4
+FP4X4 = mybir.dt.float4_e2m1fn_x4
+ALU = mybir.AluOpType
+ACT = mybir.ActivationFunctionType
+AXIS = mybir.AxisListType
+
+P = 128
+PACK = 4
+HALF = LISTED // 2
+PER_COLUMN = 16
+TERMS = 19
+WORD_LOADS = [(0, 1024), (1024, 2048)]
+PASSES = [(0, 512), (512, 1024), (1024, 1536), (1536, 1792), (1792, 1920), (1920, 2048)]
+VECTOR_SHARE = 672
+CAST_SHARE = 88
+STORES = [(0, 256, "v"), (1536, 2048, "s"), (256, 768, "v"), (768, 1536, "v")]
+EXPONENT_BITS = 0x7F800000
+SIGN_AND_EXPONENT_BITS = -0x00800000
+
+
+def tile_attend_allowedset_heads_kernel(tc, hid, voc_words, voc_scales, fine, offs, out):
+    nc = tc.nc
+    with ExitStack() as ctx:
+        keep = ctx.enter_context(tc.tile_pool(name="keep", bufs=1))
+        psum = ctx.enter_context(tc.psum_pool(name="psum", bufs=1))
+
+        offsets = keep.tile([P, LISTED // PER_COLUMN], U16, name="offsets")
+        voc_plane = keep.tile([P, V], U8, align_bytes=64, name="voc_plane")
+        nc.vector.memset(voc_plane[:].bitcast(I32), 0)
+
+        hid_rows = keep.tile([P, PACK, Q], F32, name="hid_rows", tag="hid_then_fine")
+        nc.sync.dma_start(out=hid_rows[:], in_=hid.rearrange("(p t) q -> p t q", t=PACK))
+        for quadrant in range(4):
+            nc.sync.dma_start(
+                out=voc_plane[32 * quadrant : 32 * quadrant + 4, :].bitcast(I32),
+                in_=voc_scales[0, 4 * quadrant : 4 * quadrant + 4, :].bitcast(I32),
+            )
+        words = []
+        for lo, hi in WORD_LOADS:
+            tile = keep.tile([P, 2 * (hi - lo)], U8, align_bytes=64, name="words%d" % lo)
+            nc.sync.dma_start(out=tile[:].bitcast(I32), in_=voc_words[0, :, 2 * lo : 2 * hi].bitcast(I32))
+            words.append((lo, hi, tile))
+        nc.sync.dma_start(offsets[:], offs)
+
+        placed = keep.tile([P, V], F32, name="placed")
+        nc.vector.memset(placed[:], 0.0)
+
+        order = keep.tile([P, TERMS], F32, name="order")
+        nc.gpsimd.iota(order[:], [[-1, TERMS]], base=TERMS, channel_multiplier=0, allow_small_or_imprecise_dtypes=True)
+        third_power = keep.tile([P, TERMS], F32, name="third_power")
+        nc.scalar.activation(third_power[:], order[:], ACT.Exp, scale=-math.log(3.0))
+        inverse_order = keep.tile([P, TERMS], F32, name="inverse_order")
+        nc.vector.reciprocal(inverse_order[:], order[:])
+        series = keep.tile([P, TERMS + 1], F32, name="series")
+        nc.vector.tensor_tensor(series[:, :TERMS], third_power[:], inverse_order[:], ALU.mult)
+
+        hid_grouped = keep.tile([P, Q, PACK], BF16, align_bytes=64, name="hid_grouped")
+        hid_turned = hid_rows[:].rearrange("p t q -> p q t")
+        nc.vector.tensor_copy(out=hid_grouped[:, :CAST_SHARE, :], in_=hid_turned[:, :CAST_SHARE, :])
+        nc.scalar.copy(out=hid_grouped[:, CAST_SHARE:, :], in_=hid_turned[:, CAST_SHARE:, :])
+        fine_col = keep.tile([P, 1], F32, name="fine_col", tag="hid_then_fine")
+        nc.sync.dma_start(out=fine_col[:], in_=fine)
+        hid_codes = keep.tile([P, Q], U32, align_bytes=64, name="hid_codes")
+        hid_plane = keep.tile([P, Q], U8, align_bytes=64, name="hid_plane")
+        nc.vector.quantize_mx(
+            out=hid_codes[:].bitcast(FP8X4),
+            scales=hid_plane[:],
+            in_=hid_grouped[:].rearrange("p q t -> p (q t)"),
+        )
+
+        scores = keep.tile([P, V], F32, name="scores")
+        for n, (lo, hi) in enumerate(PASSES):
+            first, last, tile = [w for w in words if w[0] <= lo and hi <= w[1]][0]
+            bank = psum.tile([P, hi - lo], F32, name="bank%d" % n)
+            nc.tensor.matmul_mx(
+                out=bank[:],
+                lhsT=hid_codes[:].bitcast(FP8X4),
+                lhsT_scale=hid_plane[:],
+                rhs=tile[:, 2 * (lo - first) : 2 * (hi - first)].bitcast(FP4X4),
+                rhs_scale=voc_plane[:, lo:hi],
+                start=True,
+                stop=True,
+            )
+            if n % 2 == 1:
+                nc.vector.tensor_copy(out=scores[:, lo:hi], in_=bank[:])
+            else:
+                nc.scalar.copy(out=scores[:, lo:hi], in_=bank[:])
+
+        picked = keep.tile([P, LISTED], F32, name="picked")
+        cols = HALF // PER_COLUMN
+        nc.vector.tensor_copy(picked[:, :HALF], scores[:].indirect(offsets[:, :cols]))
+        nc.vector.tensor_copy(picked[:, HALF:], scores[:].indirect(offsets[:, cols:]))
+
+        negated = keep.tile([P, HALF + 1], F32, name="negated")
+        neg_max_first = negated[:, HALF : HALF + 1]
+        nc.vector.tensor_reduce(neg_max_first, picked[:, :HALF], AXIS.X, ALU.max, negate=True)
+        neg_max = keep.tile([P, 1], F32, name="neg_max")
+        nc.vector.tensor_scalar(
+            negated[:, :HALF], picked[:, HALF:], -1.0, neg_max_first, ALU.mult, ALU.min, accum_out=neg_max[:]
+        )
+
+        exp_first = keep.tile([P, HALF], F32, name="exp_first")
+        sum_first = keep.tile([P, 1], F32, name="sum_first")
+        nc.scalar.activation(exp_first[:], picked[:, :HALF], ACT.Exp, bias=neg_max_first, accum_out=sum_first[:])
+        exp_second = keep.tile([P, HALF + 1], F32, name="exp_second")
+        sum_second = keep.tile([P, 1], F32, name="sum_second")
+        nc.scalar.activation(
+            exp_second[:], negated[:], ACT.Exp, bias=neg_max[:], scale=-1.0, accum_out=sum_second[:]
+        )
+        rest_first = keep.tile([P, 1], F32, name="rest_first")
+        nc.vector.tensor_scalar(rest_first[:], sum_first[:], -1.0, None, ALU.add)
+        offset = keep.tile([P, 1], F32, name="offset")
+        nc.vector.tensor_scalar(
+            offset[:], fine_col[:], neg_max[:], 129.0 * math.log(2.0) - math.log(3.0), ALU.add, ALU.add
+        )
+
+        total = keep.tile([P, 1], F32, name="total")
+        nc.vector.tensor_scalar(
+            total[:], exp_second[:, HALF : HALF + 1], rest_first[:], sum_second[:], ALU.mult, ALU.add
+        )
+        power = keep.tile([P, 1], I32, name="power")
+        nc.vector.tensor_scalar(
+            power[:], total[:].bitcast(I32), EXPONENT_BITS, SIGN_AND_EXPONENT_BITS, ALU.bitwise_and, ALU.bitwise_xor
+        )
+        distance = keep.tile([P, TERMS + 1], F32, name="distance")
+        nc.vector.tensor_scalar(
+            distance[:], total[:].to_broadcast([P, TERMS + 1]), power[:].bitcast(F32), 3.0, ALU.mult, ALU.add
+        )
+        nc.vector.tensor_scalar(
+            series[:, TERMS:], power[:], math.log(2.0) / 2.0**23, offset[:], ALU.mult, ALU.add
+        )
+        horner = keep.tile([P, TERMS + 1], F32, name="horner")
+        nc.vector.tensor_tensor_scan(horner[:], distance[:], series[:], 0.0, ALU.mult, ALU.add)
+        up = horner[:, TERMS:]
+
+        lifted = keep.tile([P, LISTED], F32, name="lifted")
+        nc.vector.tensor_scalar(lifted[:, :VECTOR_SHARE], picked[:, :VECTOR_SHARE], up, None, ALU.add)
+        nc.scalar.activation(lifted[:, VECTOR_SHARE:], picked[:, VECTOR_SHARE:], ACT.Identity, bias=up)
+        nc.vector.tensor_copy(placed[:].indirect(offsets[:]), lifted[:])
+
+        neg_fine = keep.tile([P, 1], F32, name="neg_fine")
+        nc.scalar.activation(neg_fine[:], fine_col[:], ACT.Copy, scale=-1.0)
+        for lo, hi, engine in STORES:
+            result = keep.tile([P, hi - lo], F32, name="result%d" % lo)
+            if engine == "v":
+                nc.vector.tensor_scalar(result[:], placed[:, lo:hi], neg_fine[:], None, ALU.add)
+            else:
+                nc.scalar.activation(result[:], placed[:, lo:hi], ACT.Identity, bias=neg_fine[:])
+            nc.sync.dma_start(out=out[:, lo:hi], in_=result[:])

@@ -23,10 +23,10 @@ PACK = 4
 HALF = LISTED // 2
 PER_COLUMN = 16
 TERMS = 19
-WORD_LOADS = [(0, 1024), (1024, 2048)]
-PASSES = [(0, 512), (512, 1024), (1024, 1536), (1536, 1792), (1792, 1920), (1920, 2048)]
+WORD_LOADS = [(0, 512), (512, 2048)]
+PASSES = [(0, 512, "s"), (512, 1024, "v"), (1024, 1280, "s"), (1280, 1536, "v"), (1536, 1792, "s"), (1792, 1920, "v"), (1920, 2048, "v")]
 VECTOR_SHARE = 672
-CAST_SHARE = 88
+CAST_SHARE = 22
 STORES = [(0, 256, "v"), (1536, 2048, "s"), (256, 768, "v"), (768, 1536, "v")]
 EXPONENT_BITS = 0x7F800000
 SIGN_AND_EXPONENT_BITS = -0x00800000
@@ -44,10 +44,10 @@ def tile_attend_allowedset_heads_kernel(tc, hid, voc_words, voc_scales, fine, of
 
         hid_rows = keep.tile([P, PACK, Q], F32, name="hid_rows", tag="hid_then_fine")
         nc.sync.dma_start(out=hid_rows[:], in_=hid.rearrange("(p t) q -> p t q", t=PACK))
-        for quadrant in range(4):
+        for row in range(4):
             nc.sync.dma_start(
-                out=voc_plane[32 * quadrant : 32 * quadrant + 4, :].bitcast(I32),
-                in_=voc_scales[0, 4 * quadrant : 4 * quadrant + 4, :].bitcast(I32),
+                out=voc_plane[row:P:32, :].bitcast(I32),
+                in_=voc_scales[0, row:16:4, :].bitcast(I32),
             )
         words = []
         for lo, hi in WORD_LOADS:
@@ -69,9 +69,10 @@ def tile_attend_allowedset_heads_kernel(tc, hid, voc_words, voc_scales, fine, of
         nc.vector.tensor_tensor(series[:, :TERMS], third_power[:], inverse_order[:], ALU.mult)
 
         hid_grouped = keep.tile([P, Q, PACK], BF16, align_bytes=64, name="hid_grouped")
-        hid_turned = hid_rows[:].rearrange("p t q -> p q t")
-        nc.vector.tensor_copy(out=hid_grouped[:, :CAST_SHARE, :], in_=hid_turned[:, :CAST_SHARE, :])
-        nc.scalar.copy(out=hid_grouped[:, CAST_SHARE:, :], in_=hid_turned[:, CAST_SHARE:, :])
+        hid_from = hid_rows[:].rearrange("p t (c i) -> p c t i", i=4)
+        hid_to = hid_grouped[:].rearrange("p (c i) t -> p c t i", i=4)
+        nc.vector.tensor_copy(out=hid_to[:, :CAST_SHARE], in_=hid_from[:, :CAST_SHARE])
+        nc.scalar.copy(out=hid_to[:, CAST_SHARE:], in_=hid_from[:, CAST_SHARE:])
         fine_col = keep.tile([P, 1], F32, name="fine_col", tag="hid_then_fine")
         nc.sync.dma_start(out=fine_col[:], in_=fine)
         hid_codes = keep.tile([P, Q], U32, align_bytes=64, name="hid_codes")
@@ -83,7 +84,7 @@ def tile_attend_allowedset_heads_kernel(tc, hid, voc_words, voc_scales, fine, of
         )
 
         scores = keep.tile([P, V], F32, name="scores")
-        for n, (lo, hi) in enumerate(PASSES):
+        for n, (lo, hi, engine) in enumerate(PASSES):
             first, last, tile = [w for w in words if w[0] <= lo and hi <= w[1]][0]
             bank = psum.tile([P, hi - lo], F32, name="bank%d" % n)
             nc.tensor.matmul_mx(
@@ -95,7 +96,7 @@ def tile_attend_allowedset_heads_kernel(tc, hid, voc_words, voc_scales, fine, of
                 start=True,
                 stop=True,
             )
-            if n % 2 == 1:
+            if engine == "v":
                 nc.vector.tensor_copy(out=scores[:, lo:hi], in_=bank[:])
             else:
                 nc.scalar.copy(out=scores[:, lo:hi], in_=bank[:])

@@ -20,14 +20,19 @@ AXIS = mybir.AxisListType
 
 P = 128
 PACK = 4
-HALF = LISTED // 2
+QUADRANT = 32
+SCALE_ROWS = 4
+WORD_BYTES = 2
 PER_COLUMN = 16
+HALF = LISTED // 2
 TERMS = 19
-WORD_LOADS = [(0, 512), (512, 2048)]
-PASSES = [(0, 512, "s"), (512, 1024, "v"), (1024, 1280, "s"), (1280, 1536, "v"), (1536, 1792, "s"), (1792, 1920, "v"), (1920, 2048, "v")]
-VECTOR_SHARE = 672
+
+WORD_LOADS = [(0, V // 2), (V // 2, V)]
+PASSES = [(512, "scalar"), (512, "vector"), (256, "scalar"), (256, "vector"), (256, "scalar"), (128, "vector"), (128, "vector")]
 CAST_SHARE = 22
-STORES = [(0, 256, "v"), (1536, 2048, "s"), (256, 768, "v"), (768, 1536, "v")]
+LIFT_SHARE = 672
+STORES = [(0, 256, "vector"), (1536, 2048, "scalar"), (256, 768, "vector"), (768, 1536, "vector")]
+
 EXPONENT_BITS = 0x7F800000
 SIGN_AND_EXPONENT_BITS = -0x00800000
 
@@ -44,23 +49,24 @@ def tile_attend_allowedset_heads_kernel(tc, hid, voc_words, voc_scales, fine, of
 
         hid_rows = keep.tile([P, PACK, Q], F32, name="hid_rows", tag="hid_then_fine")
         nc.sync.dma_start(out=hid_rows[:], in_=hid.rearrange("(p t) q -> p t q", t=PACK))
-        for row in range(4):
+        for row in range(SCALE_ROWS):
             nc.sync.dma_start(
-                out=voc_plane[row:P:32, :].bitcast(I32),
-                in_=voc_scales[0, row:16:4, :].bitcast(I32),
+                out=voc_plane[row:P:QUADRANT, :].bitcast(I32),
+                in_=voc_scales[0, row : D // 32 : SCALE_ROWS, :].bitcast(I32),
             )
         words = []
         for lo, hi in WORD_LOADS:
-            tile = keep.tile([P, 2 * (hi - lo)], U8, align_bytes=64, name="words%d" % lo)
-            nc.sync.dma_start(out=tile[:].bitcast(I32), in_=voc_words[0, :, 2 * lo : 2 * hi].bitcast(I32))
+            tile = keep.tile([P, WORD_BYTES * (hi - lo)], U8, align_bytes=64, name="words%d" % lo)
+            nc.sync.dma_start(
+                out=tile[:].bitcast(I32), in_=voc_words[0, :, WORD_BYTES * lo : WORD_BYTES * hi].bitcast(I32)
+            )
             words.append((lo, hi, tile))
         nc.sync.dma_start(offsets[:], offs)
 
-        placed = keep.tile([P, V], F32, name="placed")
-        nc.vector.memset(placed[:], 0.0)
-
         order = keep.tile([P, TERMS], F32, name="order")
-        nc.gpsimd.iota(order[:], [[-1, TERMS]], base=TERMS, channel_multiplier=0, allow_small_or_imprecise_dtypes=True)
+        half_step = keep.tile([P, TERMS], F32, name="half_step")
+        nc.vector.memset(half_step[:], -0.5)
+        nc.vector.tensor_tensor_scan(order[:], half_step[:], half_step[:], TERMS + 1.0, ALU.add, ALU.add)
         third_power = keep.tile([P, TERMS], F32, name="third_power")
         nc.scalar.activation(third_power[:], order[:], ACT.Exp, scale=-math.log(3.0))
         inverse_order = keep.tile([P, TERMS], F32, name="inverse_order")
@@ -68,7 +74,7 @@ def tile_attend_allowedset_heads_kernel(tc, hid, voc_words, voc_scales, fine, of
         series = keep.tile([P, TERMS + 1], F32, name="series")
         nc.vector.tensor_tensor(series[:, :TERMS], third_power[:], inverse_order[:], ALU.mult)
 
-        hid_grouped = keep.tile([P, Q, PACK], BF16, align_bytes=64, name="hid_grouped")
+        hid_grouped = keep.tile([P, Q, PACK], BF16, align_bytes=64, name="hid_grouped", tag="grouped_then_placed")
         hid_from = hid_rows[:].rearrange("p t (c i) -> p c t i", i=4)
         hid_to = hid_grouped[:].rearrange("p (c i) t -> p c t i", i=4)
         nc.vector.tensor_copy(out=hid_to[:, :CAST_SHARE], in_=hid_from[:, :CAST_SHARE])
@@ -83,37 +89,42 @@ def tile_attend_allowedset_heads_kernel(tc, hid, voc_words, voc_scales, fine, of
             in_=hid_grouped[:].rearrange("p q t -> p (q t)"),
         )
 
+        placed = keep.tile([P, V], F32, align_bytes=64, name="placed", tag="grouped_then_placed")
+        nc.gpsimd.memset(placed[:], 0.0)
+
         scores = keep.tile([P, V], F32, name="scores")
-        for n, (lo, hi, engine) in enumerate(PASSES):
-            first, last, tile = [w for w in words if w[0] <= lo and hi <= w[1]][0]
-            bank = psum.tile([P, hi - lo], F32, name="bank%d" % n)
+        lo = 0
+        for n, (width, engine) in enumerate(PASSES):
+            hi = lo + width
+            first, tile = [(w[0], w[2]) for w in words if w[0] <= lo and hi <= w[1]][0]
+            bank = psum.tile([P, width], F32, name="bank%d" % n)
             nc.tensor.matmul_mx(
                 out=bank[:],
                 lhsT=hid_codes[:].bitcast(FP8X4),
                 lhsT_scale=hid_plane[:],
-                rhs=tile[:, 2 * (lo - first) : 2 * (hi - first)].bitcast(FP4X4),
+                rhs=tile[:, WORD_BYTES * (lo - first) : WORD_BYTES * (hi - first)].bitcast(FP4X4),
                 rhs_scale=voc_plane[:, lo:hi],
                 start=True,
                 stop=True,
             )
-            if engine == "v":
+            if engine == "vector":
                 nc.vector.tensor_copy(out=scores[:, lo:hi], in_=bank[:])
             else:
                 nc.scalar.copy(out=scores[:, lo:hi], in_=bank[:])
+            lo = hi
 
         picked = keep.tile([P, LISTED], F32, name="picked")
-        cols = HALF // PER_COLUMN
-        nc.vector.tensor_copy(picked[:, :HALF], scores[:].indirect(offsets[:, :cols]))
-        nc.vector.tensor_copy(picked[:, HALF:], scores[:].indirect(offsets[:, cols:]))
+        half_columns = HALF // PER_COLUMN
+        nc.vector.tensor_copy(picked[:, :HALF], scores[:].indirect(offsets[:, :half_columns]))
+        nc.vector.tensor_copy(picked[:, HALF:], scores[:].indirect(offsets[:, half_columns:]))
 
         negated = keep.tile([P, HALF + 1], F32, name="negated")
-        neg_max_first = negated[:, HALF : HALF + 1]
+        neg_max_first = negated[:, HALF:]
         nc.vector.tensor_reduce(neg_max_first, picked[:, :HALF], AXIS.X, ALU.max, negate=True)
         neg_max = keep.tile([P, 1], F32, name="neg_max")
         nc.vector.tensor_scalar(
             negated[:, :HALF], picked[:, HALF:], -1.0, neg_max_first, ALU.mult, ALU.min, accum_out=neg_max[:]
         )
-
         exp_first = keep.tile([P, HALF], F32, name="exp_first")
         sum_first = keep.tile([P, 1], F32, name="sum_first")
         nc.scalar.activation(exp_first[:], picked[:, :HALF], ACT.Exp, bias=neg_max_first, accum_out=sum_first[:])
@@ -124,40 +135,36 @@ def tile_attend_allowedset_heads_kernel(tc, hid, voc_words, voc_scales, fine, of
         )
         rest_first = keep.tile([P, 1], F32, name="rest_first")
         nc.vector.tensor_scalar(rest_first[:], sum_first[:], -1.0, None, ALU.add)
-        offset = keep.tile([P, 1], F32, name="offset")
+        known = keep.tile([P, 1], F32, name="known")
         nc.vector.tensor_scalar(
-            offset[:], fine_col[:], neg_max[:], 129.0 * math.log(2.0) - math.log(3.0), ALU.add, ALU.add
+            known[:], fine_col[:], neg_max[:], 129.0 * math.log(2.0) - math.log(3.0), ALU.add, ALU.add
         )
-
         total = keep.tile([P, 1], F32, name="total")
-        nc.vector.tensor_scalar(
-            total[:], exp_second[:, HALF : HALF + 1], rest_first[:], sum_second[:], ALU.mult, ALU.add
-        )
+        nc.vector.tensor_scalar(total[:], exp_second[:, HALF:], rest_first[:], sum_second[:], ALU.mult, ALU.add)
+
         power = keep.tile([P, 1], I32, name="power")
         nc.vector.tensor_scalar(
             power[:], total[:].bitcast(I32), EXPONENT_BITS, SIGN_AND_EXPONENT_BITS, ALU.bitwise_and, ALU.bitwise_xor
         )
-        distance = keep.tile([P, TERMS + 1], F32, name="distance")
+        y_wide = keep.tile([P, TERMS + 1], F32, name="y_wide")
         nc.vector.tensor_scalar(
-            distance[:], total[:].to_broadcast([P, TERMS + 1]), power[:].bitcast(F32), 3.0, ALU.mult, ALU.add
+            y_wide[:], total[:].to_broadcast([P, TERMS + 1]), power[:].bitcast(F32), 3.0, ALU.mult, ALU.add
         )
-        nc.vector.tensor_scalar(
-            series[:, TERMS:], power[:], math.log(2.0) / 2.0**23, offset[:], ALU.mult, ALU.add
-        )
+        nc.vector.tensor_scalar(series[:, TERMS:], power[:], math.log(2.0) / 2.0**23, known[:], ALU.mult, ALU.add)
         horner = keep.tile([P, TERMS + 1], F32, name="horner")
-        nc.vector.tensor_tensor_scan(horner[:], distance[:], series[:], 0.0, ALU.mult, ALU.add)
+        nc.vector.tensor_tensor_scan(horner[:], y_wide[:], series[:], 0.0, ALU.mult, ALU.add)
         up = horner[:, TERMS:]
 
         lifted = keep.tile([P, LISTED], F32, name="lifted")
-        nc.vector.tensor_scalar(lifted[:, :VECTOR_SHARE], picked[:, :VECTOR_SHARE], up, None, ALU.add)
-        nc.scalar.activation(lifted[:, VECTOR_SHARE:], picked[:, VECTOR_SHARE:], ACT.Identity, bias=up)
+        nc.vector.tensor_scalar(lifted[:, :LIFT_SHARE], picked[:, :LIFT_SHARE], up, None, ALU.add)
+        nc.scalar.activation(lifted[:, LIFT_SHARE:], picked[:, LIFT_SHARE:], ACT.Identity, bias=up)
         nc.vector.tensor_copy(placed[:].indirect(offsets[:]), lifted[:])
 
         neg_fine = keep.tile([P, 1], F32, name="neg_fine")
         nc.scalar.activation(neg_fine[:], fine_col[:], ACT.Copy, scale=-1.0)
         for lo, hi, engine in STORES:
             result = keep.tile([P, hi - lo], F32, name="result%d" % lo)
-            if engine == "v":
+            if engine == "vector":
                 nc.vector.tensor_scalar(result[:], placed[:, lo:hi], neg_fine[:], None, ALU.add)
             else:
                 nc.scalar.activation(result[:], placed[:, lo:hi], ACT.Identity, bias=neg_fine[:])

@@ -27,7 +27,7 @@ PER_COLUMN = 16
 HALF = LISTED // 2
 TERMS = 19
 
-WORD_LOADS = [(0, V // 2), (V // 2, V)]
+WORD_LOADS = [(0, V // 4), (V // 4, V // 2), (V // 2, V)]
 PASSES = [(512, "scalar"), (512, "vector"), (256, "scalar"), (256, "vector"), (256, "scalar"), (128, "vector"), (128, "vector")]
 CAST_SHARE = 22
 LIFT_SHARE = 672
@@ -63,6 +63,9 @@ def tile_attend_allowedset_heads_kernel(tc, hid, voc_words, voc_scales, fine, of
             words.append((lo, hi, tile))
         nc.sync.dma_start(offsets[:], offs)
 
+        placed = keep.tile([P, V], F32, name="placed")
+        nc.vector.memset(placed[:].bitcast(I32), 0)
+
         order = keep.tile([P, TERMS], F32, name="order")
         half_step = keep.tile([P, TERMS], F32, name="half_step")
         nc.vector.memset(half_step[:], -0.5)
@@ -74,7 +77,7 @@ def tile_attend_allowedset_heads_kernel(tc, hid, voc_words, voc_scales, fine, of
         series = keep.tile([P, TERMS + 1], F32, name="series")
         nc.vector.tensor_tensor(series[:, :TERMS], third_power[:], inverse_order[:], ALU.mult)
 
-        hid_grouped = keep.tile([P, Q, PACK], BF16, align_bytes=64, name="hid_grouped", tag="grouped_then_placed")
+        hid_grouped = keep.tile([P, Q, PACK], BF16, align_bytes=64, name="hid_grouped")
         hid_from = hid_rows[:].rearrange("p t (c i) -> p c t i", i=4)
         hid_to = hid_grouped[:].rearrange("p (c i) t -> p c t i", i=4)
         nc.vector.tensor_copy(out=hid_to[:, :CAST_SHARE], in_=hid_from[:, :CAST_SHARE])
@@ -88,9 +91,6 @@ def tile_attend_allowedset_heads_kernel(tc, hid, voc_words, voc_scales, fine, of
             scales=hid_plane[:],
             in_=hid_grouped[:].rearrange("p q t -> p (q t)"),
         )
-
-        placed = keep.tile([P, V], F32, align_bytes=64, name="placed", tag="grouped_then_placed")
-        nc.gpsimd.memset(placed[:], 0.0)
 
         scores = keep.tile([P, V], F32, name="scores")
         lo = 0

import math
from contextlib import ExitStack

import concourse.mybir as mybir

D, V, Q, LISTED = 512, 2048, 128, 1024
FLOPS = 2 * D * V * Q

F32 = mybir.dt.float32
BF16 = mybir.dt.bfloat16
I32 = mybir.dt.int32
U32 = mybir.dt.uint32
U16 = mybir.dt.uint16
U8 = mybir.dt.uint8
FP8X4 = mybir.dt.float8_e4m3fn_x4
FP4X4 = mybir.dt.float4_e2m1fn_x4
ALU = mybir.AluOpType
ACT = mybir.ActivationFunctionType
AXIS = mybir.AxisListType

P = 128
PACK = 4
QUADRANT = 32
SCALE_ROWS = 4
WORD_BYTES = 2
PER_COLUMN = 16
HALF = LISTED // 2
TERMS = 19

WORD_LOADS = [(0, V // 4), (V // 4, V // 2), (V // 2, V)]
PASSES = [(512, "scalar"), (512, "vector"), (256, "scalar"), (256, "vector"), (256, "scalar"), (128, "vector"), (128, "vector")]
CAST_SHARE = 22
LIFT_SHARE = 672
STORES = [(0, 256, "vector"), (1536, 2048, "scalar"), (256, 768, "vector"), (768, 1536, "vector")]

EXPONENT_BITS = 0x7F800000
SIGN_AND_EXPONENT_BITS = -0x00800000


def tile_attend_allowedset_heads_kernel(tc, hid, voc_words, voc_scales, fine, offs, out):
    nc = tc.nc
    with ExitStack() as ctx:
        keep = ctx.enter_context(tc.tile_pool(name="keep", bufs=1))
        psum = ctx.enter_context(tc.psum_pool(name="psum", bufs=1))

        offsets = keep.tile([P, LISTED // PER_COLUMN], U16, name="offsets")
        voc_plane = keep.tile([P, V], U8, align_bytes=64, name="voc_plane")
        nc.vector.memset(voc_plane[:].bitcast(I32), 0)

        hid_rows = keep.tile([P, PACK, Q], F32, name="hid_rows", tag="hid_then_fine")
        nc.sync.dma_start(out=hid_rows[:], in_=hid.rearrange("(p t) q -> p t q", t=PACK))
        for row in range(SCALE_ROWS):
            nc.sync.dma_start(
                out=voc_plane[row:P:QUADRANT, :].bitcast(I32),
                in_=voc_scales[0, row : D // 32 : SCALE_ROWS, :].bitcast(I32),
            )
        words = []
        for lo, hi in WORD_LOADS:
            tile = keep.tile([P, WORD_BYTES * (hi - lo)], U8, align_bytes=64, name="words%d" % lo)
            nc.sync.dma_start(
                out=tile[:].bitcast(I32), in_=voc_words[0, :, WORD_BYTES * lo : WORD_BYTES * hi].bitcast(I32)
            )
            words.append((lo, hi, tile))
        nc.sync.dma_start(offsets[:], offs)

        placed = keep.tile([P, V], F32, name="placed")
        nc.vector.memset(placed[:].bitcast(I32), 0)

        order = keep.tile([P, TERMS], F32, name="order")
        half_step = keep.tile([P, TERMS], F32, name="half_step")
        nc.vector.memset(half_step[:], -0.5)
        nc.vector.tensor_tensor_scan(order[:], half_step[:], half_step[:], TERMS + 1.0, ALU.add, ALU.add)
        third_power = keep.tile([P, TERMS], F32, name="third_power")
        nc.scalar.activation(third_power[:], order[:], ACT.Exp, scale=-math.log(3.0))
        inverse_order = keep.tile([P, TERMS], F32, name="inverse_order")
        nc.vector.reciprocal(inverse_order[:], order[:])
        series = keep.tile([P, TERMS + 1], F32, name="series")
        nc.vector.tensor_tensor(series[:, :TERMS], third_power[:], inverse_order[:], ALU.mult)

        hid_grouped = keep.tile([P, Q, PACK], BF16, align_bytes=64, name="hid_grouped")
        hid_from = hid_rows[:].rearrange("p t (c i) -> p c t i", i=4)
        hid_to = hid_grouped[:].rearrange("p (c i) t -> p c t i", i=4)
        nc.vector.tensor_copy(out=hid_to[:, :CAST_SHARE], in_=hid_from[:, :CAST_SHARE])
        nc.scalar.copy(out=hid_to[:, CAST_SHARE:], in_=hid_from[:, CAST_SHARE:])
        fine_col = keep.tile([P, 1], F32, name="fine_col", tag="hid_then_fine")
        nc.sync.dma_start(out=fine_col[:], in_=fine)
        hid_codes = keep.tile([P, Q], U32, align_bytes=64, name="hid_codes")
        hid_plane = keep.tile([P, Q], U8, align_bytes=64, name="hid_plane")
        nc.vector.quantize_mx(
            out=hid_codes[:].bitcast(FP8X4),
            scales=hid_plane[:],
            in_=hid_grouped[:].rearrange("p q t -> p (q t)"),
        )

        scores = keep.tile([P, V], F32, name="scores")
        lo = 0
        for n, (width, engine) in enumerate(PASSES):
            hi = lo + width
            first, tile = [(w[0], w[2]) for w in words if w[0] <= lo and hi <= w[1]][0]
            bank = psum.tile([P, width], F32, name="bank%d" % n)
            nc.tensor.matmul_mx(
                out=bank[:],
                lhsT=hid_codes[:].bitcast(FP8X4),
                lhsT_scale=hid_plane[:],
                rhs=tile[:, WORD_BYTES * (lo - first) : WORD_BYTES * (hi - first)].bitcast(FP4X4),
                rhs_scale=voc_plane[:, lo:hi],
                start=True,
                stop=True,
            )
            if engine == "vector":
                nc.vector.tensor_copy(out=scores[:, lo:hi], in_=bank[:])
            else:
                nc.scalar.copy(out=scores[:, lo:hi], in_=bank[:])
            lo = hi

        picked = keep.tile([P, LISTED], F32, name="picked")
        half_columns = HALF // PER_COLUMN
        nc.vector.tensor_copy(picked[:, :HALF], scores[:].indirect(offsets[:, :half_columns]))
        nc.vector.tensor_copy(picked[:, HALF:], scores[:].indirect(offsets[:, half_columns:]))

        negated = keep.tile([P, HALF + 1], F32, name="negated")
        neg_max_first = negated[:, HALF:]
        nc.vector.tensor_reduce(neg_max_first, picked[:, :HALF], AXIS.X, ALU.max, negate=True)
        neg_max = keep.tile([P, 1], F32, name="neg_max")
        nc.vector.tensor_scalar(
            negated[:, :HALF], picked[:, HALF:], -1.0, neg_max_first, ALU.mult, ALU.min, accum_out=neg_max[:]
        )
        exp_first = keep.tile([P, HALF], F32, name="exp_first")
        sum_first = keep.tile([P, 1], F32, name="sum_first")
        nc.scalar.activation(exp_first[:], picked[:, :HALF], ACT.Exp, bias=neg_max_first, accum_out=sum_first[:])
        exp_second = keep.tile([P, HALF + 1], F32, name="exp_second")
        sum_second = keep.tile([P, 1], F32, name="sum_second")
        nc.scalar.activation(
            exp_second[:], negated[:], ACT.Exp, bias=neg_max[:], scale=-1.0, accum_out=sum_second[:]
        )
        rest_first = keep.tile([P, 1], F32, name="rest_first")
        nc.vector.tensor_scalar(rest_first[:], sum_first[:], -1.0, None, ALU.add)
        known = keep.tile([P, 1], F32, name="known")
        nc.vector.tensor_scalar(
            known[:], fine_col[:], neg_max[:], 129.0 * math.log(2.0) - math.log(3.0), ALU.add, ALU.add
        )
        total = keep.tile([P, 1], F32, name="total")
        nc.vector.tensor_scalar(total[:], exp_second[:, HALF:], rest_first[:], sum_second[:], ALU.mult, ALU.add)

        power = keep.tile([P, 1], I32, name="power")
        nc.vector.tensor_scalar(
            power[:], total[:].bitcast(I32), EXPONENT_BITS, SIGN_AND_EXPONENT_BITS, ALU.bitwise_and, ALU.bitwise_xor
        )
        y_wide = keep.tile([P, TERMS + 1], F32, name="y_wide")
        nc.vector.tensor_scalar(
            y_wide[:], total[:].to_broadcast([P, TERMS + 1]), power[:].bitcast(F32), 3.0, ALU.mult, ALU.add
        )
        nc.vector.tensor_scalar(series[:, TERMS:], power[:], math.log(2.0) / 2.0**23, known[:], ALU.mult, ALU.add)
        horner = keep.tile([P, TERMS + 1], F32, name="horner")
        nc.vector.tensor_tensor_scan(horner[:], y_wide[:], series[:], 0.0, ALU.mult, ALU.add)
        up = horner[:, TERMS:]

        lifted = keep.tile([P, LISTED], F32, name="lifted")
        nc.vector.tensor_scalar(lifted[:, :LIFT_SHARE], picked[:, :LIFT_SHARE], up, None, ALU.add)
        nc.scalar.activation(lifted[:, LIFT_SHARE:], picked[:, LIFT_SHARE:], ACT.Identity, bias=up)
        nc.vector.tensor_copy(placed[:].indirect(offsets[:]), lifted[:])

        neg_fine = keep.tile([P, 1], F32, name="neg_fine")
        nc.scalar.activation(neg_fine[:], fine_col[:], ACT.Copy, scale=-1.0)
        for lo, hi, engine in STORES:
            result = keep.tile([P, hi - lo], F32, name="result%d" % lo)
            if engine == "vector":
                nc.vector.tensor_scalar(result[:], placed[:, lo:hi], neg_fine[:], None, ALU.add)
            else:
                nc.scalar.activation(result[:], placed[:, lo:hi], ACT.Identity, bias=neg_fine[:])
            nc.sync.dma_start(out=out[:, lo:hi], in_=result[:])
